import numpy as np
import ml_dtypes


def mxq(x, axis, fmt="e4m3"):
    dtype, down = {"e4m3": (ml_dtypes.float8_e4m3fn, 7), "e5m2": (ml_dtypes.float8_e5m2, 14)}[fmt]
    v = np.moveaxis(np.asarray(x, np.float32).astype(ml_dtypes.bfloat16).astype(np.float64), axis, -1)
    blocks = v.reshape(v.shape[:-1] + (-1, 32))
    amax = np.abs(blocks).max(-1, keepdims=True)
    byte = np.maximum(np.where(amax > 0, np.frexp(amax)[1] - 1 + 127, 0) - down, 1)
    scale = np.exp2(byte - 127.0)
    codes = (blocks / scale).astype(np.float32).astype(dtype).astype(np.float64)
    return np.moveaxis((codes * scale).reshape(v.shape), -1, axis)


WIDE = False


def mx_kscale(k):
    if not WIDE:
        return np.ones(k)
    levels = np.array([10, -10, 5, -5, 0])
    if k % 512:
        return np.exp2(np.random.permutation(np.resize(levels, k // 32))).repeat(32)
    a = np.empty((k // 512, 16))
    for p in range(k // 512):
        a[p, :8] = np.random.permutation(np.resize(levels, 8))
        for g in range(8):
            far = levels[np.abs(levels - a[p, g]) >= 10]
            a[p, g + 8] = far[np.random.randint(len(far))]
    return np.exp2(a.ravel()).repeat(32)


def f64(x):
    return np.asarray(x).astype(np.float64)


def striped(idx):
    return np.tile(idx.reshape(-1, 16).T, (8, 1)).astype(np.uint16)


def unstriped(offs):
    return offs[:16].T.reshape(-1).astype(np.int64)


E2M1 = np.array([0.0, 0.5, 1.0, 1.5, 2.0, 3.0, 4.0, 6.0, -0.0, -0.5, -1.0, -1.5, -2.0, -3.0, -4.0, -6.0])


def pack_weight(w, fmt):
    k, n = w.shape
    w = f64(np.asarray(w, np.float32).astype(ml_dtypes.bfloat16)).reshape(k // 32, 32, n)
    amax = np.abs(w).max(1)
    if fmt == "e4m3":
        byte = np.frexp(amax)[1] - 1 + 127 - 7
    else:
        mant, ex = np.frexp(amax / 6.0)
        byte = np.where(mant > 0.5, ex, ex - 1) + 127
    byte = np.clip(np.where(amax > 0, byte, 1), 1, 254)
    scaled = (w * np.exp2(127.0 - byte)[:, None, :]).reshape(k, n).astype(np.float32)
    by_word = np.ascontiguousarray(scaled.reshape(k // 512, 128, 4, n).transpose(0, 1, 3, 2))
    if fmt == "e4m3":
        words = by_word.astype(ml_dtypes.float8_e4m3fn).view(np.uint8)
    else:
        c = by_word.astype(ml_dtypes.float4_e2m1fn).view(np.uint8) & 0xF
        words = (c[..., 0::2] | (c[..., 1::2] << 4)).reshape(k // 512, 128, 2 * n)
    return np.ascontiguousarray(words), np.ascontiguousarray(byte.astype(np.uint8).reshape(k // 512, 16, n))


def unpack_weight(words, scales, fmt):
    g, _, n = scales.shape
    words = np.ascontiguousarray(words).reshape(g, 128, n, -1)
    if fmt == "e4m3":
        vals = words.view(ml_dtypes.float8_e4m3fn).astype(np.float64)
    else:
        nib = np.empty((g, 128, n, 4), np.uint8)
        nib[..., 0::2] = words & 0xF
        nib[..., 1::2] = words >> 4
        vals = E2M1[nib]
    vals = vals * np.repeat(np.exp2(scales.astype(np.float64) - 127.0), 8, axis=1)[..., None]
    return vals.transpose(0, 1, 3, 2).reshape(g * 512, n)


def gelu(v):
    return 0.5 * v * (1.0 + np.tanh(np.sqrt(2.0 / np.pi) * (v + 0.044715 * v**3)))


def bf(x):
    return np.asarray(x, np.float32).astype(ml_dtypes.bfloat16)


def planes(Y):
    n, m = Y.shape
    b = f64(bf(Y)).reshape(n // 32, 32, m)
    amax = np.abs(b).max(1)
    byte = np.clip(np.where(amax > 0, np.frexp(amax)[1] - 1 + 127 - 7, 1), 1, 254)
    codes = (b * np.exp2(127.0 - byte)[:, None, :]).reshape(n, m).astype(np.float32).astype(ml_dtypes.float8_e4m3fn).view(np.uint8)
    words = codes.reshape(n // 512, 128, 4, m).transpose(0, 1, 3, 2)
    return np.ascontiguousarray(words), np.ascontiguousarray(byte.astype(np.uint8).reshape(n // 512, 16, m))


K, T, S, H, N, P = 1536, 2048, 1024, 1024, 512, 512


def setup_inputs():
    n = np.random.standard_normal
    s = mx_kscale(K)[:, None]
    u = mx_kscale(H)[:, None]
    tab_words, tab_scales = pack_weight(n((K, T)) * s, "e4m3")
    wa_words, wa_scales = pack_weight(1.2 * n((H, N)) / np.sqrt(H) / u, "e2m1")
    return {
        "tab_words": tab_words,
        "tab_scales": tab_scales,
        "offs": striped(np.random.permutation(T)[:S]),
        "pos1": striped(np.random.permutation(S)[:P]),
        "pos2": striped(np.random.permutation(S)[:P]),
        "w1": (n((K, H)) / np.sqrt(K) / s * u.T).astype(np.float32),
        "b1": (0.5 * n(H) * u[:, 0]).astype(np.float32),
        "wa_words": wa_words,
        "wa_scales": wa_scales,
        "wb": (n((H, N)) / np.sqrt(H) / u).astype(np.float32),
        "limit": n(N).astype(np.float32),
        "gm": (2.2 * n((N, P))).astype(np.float32),
        "gain": np.exp(0.8 * n(N)).astype(np.float32),
    }


def reference(tab_words, tab_scales, offs, pos1, pos2, w1, b1, wa_words, wa_scales, wb, limit, gm, gain):
    v = unpack_weight(tab_words, tab_scales, "e4m3")[:, unstriped(offs)]
    wa = unpack_weight(wa_words, wa_scales, "e2m1")
    h = np.maximum((mxq(f64(w1), 0, "e4m3").T @ v) + f64(b1)[:, None], 0.0)
    hq = mxq(h, 0, "e4m3")
    e = wa.T @ hq
    d = mxq(f64(wb), 0, "e4m3").T @ hq
    a = 1.0 / (1.0 + np.exp(-(e[:, unstriped(pos1)] + f64(limit)[:, None])))
    c = d[:, unstriped(pos2)]
    y = f64(gain)[:, None] * (c - a * f64(gm))
    words, scales = planes(y)
    return y, words, scales

@@ -1,0 +1,289 @@
+from contextlib import ExitStack
+
+import concourse.mybir as mybir
+
+K, T, S, H, N, M = 1536, 2048, 1024, 1024, 512, 512
+FLOPS = 2 * K * H * S + 2 * 2 * H * N * S
+
+F32 = mybir.dt.float32
+BF16 = mybir.dt.bfloat16
+I32 = mybir.dt.int32
+U32 = mybir.dt.uint32
+U16 = mybir.dt.uint16
+U8 = mybir.dt.uint8
+FP8X4 = mybir.dt.float8_e4m3fn_x4
+FP4X4 = mybir.dt.float4_e2m1fn_x4
+ACT = mybir.ActivationFunctionType
+ALU = mybir.AluOpType
+
+P = 128
+PACK = 4
+G = P * PACK
+W = 512
+KA = K // G
+HB = H // G
+JH = S // W
+V, A = "vector", "scalar"
+WARM = 0
+W1 = [[(A, A), (V, A), (V, A)], [(V, V), (V, V), (V, A)]]
+HG00 = V
+DEARLY = 2
+YS = 352
+HG01 = V
+WB = [(V, V), (A, V)]
+EE = [[A, A, A, A], [A, A, A, A]]
+DE = [[V, V, A, A], [V, V, A, A]]
+SC = [V, V, V, V]
+
+
+def copy_on(nc, engine, out, in_):
+    if engine == "vector":
+        nc.vector.tensor_copy(out=out, in_=in_)
+    else:
+        nc.scalar.copy(out=out, in_=in_)
+
+
+def tile_list_victim_destination_scores_kernel(
+    tc, tab_words, tab_scales, offs, pos1, pos2, w1, b1, wa_words, wa_scales, wb, limit, gm, gain, out_0, out_1, out_2
+):
+    nc = tc.nc
+    with ExitStack() as ctx:
+        keep = ctx.enter_context(tc.tile_pool(name="keep", bufs=1))
+        psum = ctx.enter_context(tc.psum_pool(name="psum", bufs=8))
+
+        def sb(name, shape, dtype, tag="", bufs=1):
+            return keep.tile(shape, dtype, name=name, tag=tag or name, bufs=bufs, align_bytes=64)
+
+        offs_t = keep.tile([P, S // 16], U16, name="offs_t")
+        pos1_t = keep.tile([P, M // 16], U16, name="pos1_t")
+        pos2_t = keep.tile([P, M // 16], U16, name="pos2_t")
+
+        if WARM:
+            warm = sb("warm", [P, 2], F32)
+            nc.gpsimd.memset(warm[:, 0:1], 0.0)
+            nc.scalar.activation(out=warm[:, 1:2], in_=warm[:, 0:1], func=ACT.Sigmoid)
+        tab_s = sb("tab_s", [P, T], U8)
+        wa_s_raw = sb("wa_s_raw", [P, HB, N], U8)
+        nc.gpsimd.memset(tab_s[:, 0 : T // 2].bitcast(I32), 0)
+        nc.vector.memset(tab_s[:, T // 2 : T].bitcast(I32), 0)
+        nc.gpsimd.memset(wa_s_raw[:].bitcast(I32), 0)
+
+        def load_rows(name, rows, slot):
+            raw = sb(name, [P, PACK, W], F32, tag=f"raw{slot}")
+            nc.sync.dma_start(out=raw[:], in_=rows.rearrange("(p j) c -> p j c", j=PACK))
+            return raw
+
+        nc.sync.dma_start(offs_t[:], offs)
+        wa_w_raw = sb("wa_w_raw", [P, HB, 2 * N], U8)
+        nc.sync.dma_start(out=wa_w_raw[:].bitcast(I32), in_=wa_words.rearrange("b p c -> p b c").bitcast(I32))
+        def load_table(a):
+            words = sb(f"tab_w{a}", [P, T], U32)
+            nc.sync.dma_start(out=words[:].bitcast(I32), in_=tab_words[a].rearrange("p t i -> p (t i)").bitcast(I32))
+            return words
+
+        def load_w1(b, a):
+            return load_rows(f"w1_raw_{b}_{a}", w1[a * G : (a + 1) * G, b * G : (b + 1) * G], b * KA + a)
+
+        tab_w = [load_table(0), load_table(1)]
+        for q in range(4):
+            nc.sync.dma_start(
+                out=tab_s[32 * q : 32 * q + 4 * KA, :].bitcast(I32),
+                in_=tab_scales[:, 4 * q : 4 * q + 4, :].bitcast(I32),
+            )
+        w1_raw = {(0, 0): load_w1(0, 0), (0, 1): load_w1(0, 1)}
+        for q in range(4):
+            nc.sync.dma_start(
+                out=wa_s_raw[32 * q : 32 * q + 4, :, :].bitcast(I32),
+                in_=wa_scales[:, 4 * q : 4 * q + 4, :].rearrange("b r n -> r b n").bitcast(I32),
+            )
+        tab_w.append(load_table(2))
+        w1_raw[0, 2] = load_w1(0, 2)
+        b1_t = sb("b1_t", [P, HB, PACK], F32)
+        nc.sync.dma_start(out=b1_t[:], in_=b1.rearrange("(b p t) -> p b t", b=HB, t=PACK))
+        for a in range(KA):
+            w1_raw[1, a] = load_w1(1, a)
+        wb_raw = [load_rows(f"wb_raw_{b}", wb[b * G : (b + 1) * G, :], b) for b in range(HB)]
+        nc.sync.dma_start(pos1_t[:], pos1)
+        nc.sync.dma_start(pos2_t[:], pos2)
+        limit_t = sb("limit_t", [P, PACK], F32)
+        gain_t = sb("gain_t", [P, PACK], F32)
+        nc.sync.dma_start(out=limit_t[:], in_=limit.rearrange("(p t) -> p t", t=PACK))
+        nc.sync.dma_start(out=gain_t[:], in_=gain.rearrange("(p t) -> p t", t=PACK))
+        gm_t = load_rows("gm_t", gm, 2)
+
+        wa_w = sb("wa_w", [P, HB, PACK, P, 2], U8)
+        wa_s = sb("wa_s", [P, HB, PACK, P], U8)
+        nc.vector.tensor_copy(out=wa_w[:], in_=wa_w_raw[:].rearrange("p b (m t y) -> p b t m y", t=PACK, y=2))
+
+        def round_weight(name, raw, u, engine):
+            grouped = sb(f"{name}_g{u}", [P, 2, P, PACK], BF16, tag="w_g", bufs=6)
+            copy_on(
+                nc,
+                engine,
+                grouped[:].rearrange("p t m j -> p m j t"),
+                raw[:].rearrange("p j (m t) -> p m j t", t=PACK)[:, :, :, 2 * u : 2 * u + 2],
+            )
+            return grouped
+
+        def quantize(name, grouped, width):
+            codes = sb(f"{name}_c", [P, width], U32)
+            scales = sb(f"{name}_s", [P, width], U8)
+            nc.vector.quantize_mx(out=codes[:].bitcast(FP8X4), scales=scales[:], in_=grouped)
+            return codes, scales
+
+        def quantize_weight(name, raw, engines):
+            grouped = [round_weight(name, raw, u, engines[u]) for u in range(2)]
+            return [quantize(f"{name}_{u}", grouped[u][:].rearrange("p t m j -> p (t m j)"), 2 * P) for u in range(2)]
+
+        def slice_of(quantized, t):
+            codes, scales = quantized[t // 2]
+            cols = slice((t % 2) * P, (t % 2 + 1) * P)
+            return codes[:, cols].bitcast(FP8X4), scales[:, cols]
+
+        def list_half(jh):
+            return offs_t[:, jh * (W // 16) : (jh + 1) * (W // 16)]
+
+        v_s = []
+        v_w = {}
+
+        def gather_scales(jh):
+            picked = sb(f"v_s{jh}", [P, W], U8)
+            nc.vector.tensor_copy(out=picked[:], in_=tab_s[:].indirect(list_half(jh)))
+            v_s.append(picked)
+
+        def gather_words(a, jh):
+            picked = sb(f"v_w{a}_{jh}", [P, W], U32)
+            nc.vector.tensor_copy(out=picked[:], in_=tab_w[a][:].indirect(list_half(jh)))
+            v_w[a, jh] = picked
+
+        h_acc = {}
+
+        def stage1_pass(b, a, jh):
+            for t in range(PACK):
+                if a == 0:
+                    h_acc[b, jh, t] = psum.tile([P, W], F32, name="bank")
+                lhs, lhs_s = slice_of(w1_q[b, a], t)
+                nc.tensor.matmul_mx(
+                    out=h_acc[b, jh, t][:],
+                    lhsT=lhs,
+                    lhsT_scale=lhs_s,
+                    rhs=v_w[a, jh][:].bitcast(FP8X4),
+                    rhs_scale=v_s[jh][4 * a : P, :],
+                    start=(a == 0),
+                    stop=(a == KA - 1),
+                )
+
+        h_rows = {}
+        h_q = {}
+
+        def h_out(b, jh):
+            rows = sb(f"h_rows{b}_{jh}", [P, PACK, W], BF16)
+            for t in range(PACK):
+                nc.scalar.activation(out=rows[:, t, :], in_=h_acc[b, jh, t][:], func=ACT.Relu, bias=b1_t[:, b, t : t + 1])
+            h_rows[b, jh] = rows
+
+        def interleave(name, rows, engine):
+            grouped = sb(name, [P, W, PACK], BF16, tag="x_g", bufs=2)
+            copy_on(
+                nc,
+                engine,
+                grouped[:].rearrange("p (c i) t -> p c t i", i=4),
+                rows[:].rearrange("p t (c i) -> p c t i", i=4),
+            )
+            return grouped[:].rearrange("p n t -> p (n t)")
+
+        def h_quantize(b, jh, engine):
+            h_q[b, jh] = quantize(f"h_q{b}_{jh}", interleave(f"h_g{b}_{jh}", h_rows[b, jh], engine), W)
+
+        w1_q = {}
+        for a in range(2):
+            for jh in range(JH):
+                gather_words(a, jh)
+        for jh in range(JH):
+            gather_scales(jh)
+        for a in range(KA):
+            if a == 2:
+                for jh in range(JH):
+                    gather_words(2, jh)
+            w1_q[0, a] = quantize_weight(f"w1_0_{a}", w1_raw[0, a], W1[0][a])
+            for jh in range(JH):
+                stage1_pass(0, a, jh)
+        nc.vector.tensor_copy(out=wa_s[:], in_=wa_s_raw[:].rearrange("p b (m t) -> p b t m", t=PACK))
+        for jh in range(JH):
+            h_out(0, jh)
+        for a in range(KA):
+            w1_q[1, a] = quantize_weight(f"w1_1_{a}", w1_raw[1, a], W1[1][a])
+        for jh in range(JH):
+            for a in range(KA):
+                stage1_pass(1, a, jh)
+        h_out(1, 0)
+        h_quantize(0, 0, HG00)
+        h_quantize(1, 0, V)
+        h_out(1, 1)
+        h_quantize(0, 1, HG01)
+        h_quantize(1, 1, V)
+        wb_q = [quantize_weight(f"wb_{b}", wb_raw[b], WB[b]) for b in range(HB)]
+
+        e = [sb(f"e{t}", [P, S], F32) for t in range(PACK)]
+        d = [sb(f"d{t}", [P, S], F32) for t in range(PACK)]
+
+        def stage2(whole, stationary, jh, t, engine):
+            acc = psum.tile([P, W], F32, name="bank")
+            for b in range(HB):
+                lhs, lhs_s = stationary(b, t)
+                nc.tensor.matmul_mx(
+                    out=acc[:],
+                    lhsT=lhs,
+                    lhsT_scale=lhs_s,
+                    rhs=h_q[b, jh][0][:].bitcast(FP8X4),
+                    rhs_scale=h_q[b, jh][1][:],
+                    start=(b == 0),
+                    stop=(b == HB - 1),
+                )
+            copy_on(nc, engine, whole[t][:, jh * W : (jh + 1) * W], acc[:])
+
+        def wa_slice(b, t):
+            return wa_w[:, b, t, :, :].rearrange("p m y -> p (m y)").bitcast(FP4X4), wa_s[:, b, t, :]
+
+        def wb_slice(b, t):
+            return slice_of(wb_q[b], t)
+
+        y = sb("y", [P, PACK, M], F32)
+        y_out = out_0.rearrange("(p t) m -> p t m", t=PACK)
+        for t in range(PACK):
+            stage2(e, wa_slice, 0, t, EE[0][t])
+        looks = []
+        for t in range(PACK):
+            stage2(e, wa_slice, 1, t, EE[1][t])
+            look = sb(f"look{t}", [P, M], F32)
+            nc.scalar.activation(out=look[:], in_=e[t][:].indirect(pos1_t[:]), func=ACT.Sigmoid, bias=limit_t[:, t : t + 1])
+            looks.append(look)
+            if t < DEARLY:
+                for jh in range(JH):
+                    stage2(d, wb_slice, jh, t, DE[jh][t])
+        for t in range(PACK):
+            if t >= DEARLY:
+                for jh in range(JH):
+                    stage2(d, wb_slice, jh, t, DE[jh][t])
+            signed = sb(f"cost{t}", [P, M], F32, tag="cost", bufs=2)
+            nc.vector.tensor_tensor(out=signed[:], in0=looks[t][:], in1=gm_t[:, t, :], op=ALU.mult)
+            diff = sb(f"diff{t}", [P, M], F32, tag="diff", bufs=2)
+            nc.vector.tensor_tensor(out=diff[:], in0=d[t][:].indirect(pos2_t[:]), in1=signed[:], op=ALU.subtract)
+            if SC[t] == "vector":
+                nc.vector.tensor_scalar(out=y[:, t, :], in0=diff[:], scalar1=gain_t[:, t : t + 1], scalar2=None, op0=ALU.mult)
+            else:
+                nc.scalar.activation(out=y[:, t, :], in_=diff[:], func=ACT.Copy, scale=gain_t[:, t : t + 1])
+            nc.sync.dma_start(out=y_out[:, t, :], in_=y[:, t, :])
+        y_g = sb("y_g", [P, M, PACK], BF16, tag="x_g", bufs=2)
+        for engine, cols in (("vector", slice(0, YS)), ("scalar", slice(YS, M))):
+            copy_on(
+                nc,
+                engine,
+                y_g[:, cols, :].rearrange("p (c i) t -> p c t i", i=4),
+                y[:, :, cols].rearrange("p t (c i) -> p c t i", i=4),
+            )
+        y_c, y_s = quantize("y_q", y_g[:].rearrange("p n t -> p (n t)"), M)
+        nc.sync.dma_start(out=out_1[0].rearrange("p m t -> p (m t)").bitcast(I32), in_=y_c[:].bitcast(I32))
+        for q in range(4):
+            queue = nc.scalar if q % 2 == 0 else nc.sync
+            queue.dma_start(out=out_2[0, 4 * q : 4 * q + 4, :].bitcast(I32), in_=y_s[32 * q : 32 * q + 4, :].bitcast(I32))

@@ -25,10 +25,9 @@ HB = H // G
 JH = S // W
 V, A = "vector", "scalar"
 WARM = 0
-W1 = [[(A, A), (V, A), (V, A)], [(V, V), (V, V), (V, A)]]
+W1 = [[(A, A), (A, A), (V, A)], [(V, V), (V, V), (V, A)]]
 HG00 = V
 DEARLY = 2
-YS = 352
 HG01 = V
 WB = [(V, V), (A, V)]
 EE = [[A, A, A, A], [A, A, A, A]]
@@ -64,9 +63,13 @@ def tile_list_victim_destination_scores_kernel(
             nc.scalar.activation(out=warm[:, 1:2], in_=warm[:, 0:1], func=ACT.Sigmoid)
         tab_s = sb("tab_s", [P, T], U8)
         wa_s_raw = sb("wa_s_raw", [P, HB, N], U8)
-        nc.gpsimd.memset(tab_s[:, 0 : T // 2].bitcast(I32), 0)
-        nc.vector.memset(tab_s[:, T // 2 : T].bitcast(I32), 0)
-        nc.gpsimd.memset(wa_s_raw[:].bitcast(I32), 0)
+        nc.gpsimd.memset(tab_s[:].bitcast(I32), 0)
+        nc.vector.memset(wa_s_raw[:].bitcast(I32), 0)
+        for q in range(4):
+            nc.gpsimd.dma_start(
+                out=tab_s[32 * q : 32 * q + 4 * KA, :].bitcast(I32),
+                in_=tab_scales[:, 4 * q : 4 * q + 4, :].bitcast(I32),
+            )
 
         def load_rows(name, rows, slot):
             raw = sb(name, [P, PACK, W], F32, tag=f"raw{slot}")
@@ -85,11 +88,6 @@ def tile_list_victim_destination_scores_kernel(
             return load_rows(f"w1_raw_{b}_{a}", w1[a * G : (a + 1) * G, b * G : (b + 1) * G], b * KA + a)
 
         tab_w = [load_table(0), load_table(1)]
-        for q in range(4):
-            nc.sync.dma_start(
-                out=tab_s[32 * q : 32 * q + 4 * KA, :].bitcast(I32),
-                in_=tab_scales[:, 4 * q : 4 * q + 4, :].bitcast(I32),
-            )
         w1_raw = {(0, 0): load_w1(0, 0), (0, 1): load_w1(0, 1)}
         for q in range(4):
             nc.sync.dma_start(
@@ -274,16 +272,20 @@ def tile_list_victim_destination_scores_kernel(
             else:
                 nc.scalar.activation(out=y[:, t, :], in_=diff[:], func=ACT.Copy, scale=gain_t[:, t : t + 1])
             nc.sync.dma_start(out=y_out[:, t, :], in_=y[:, t, :])
-        y_g = sb("y_g", [P, M, PACK], BF16, tag="x_g", bufs=2)
-        for engine, cols in (("vector", slice(0, YS)), ("scalar", slice(YS, M))):
+        y_c = sb("y_c", [P, M], U32)
+        y_s = sb("y_s", [P, M], U8)
+        words_out = out_1[0].rearrange("p m t -> p (m t)").bitcast(I32)
+        for half, engine in enumerate((V, A)):
+            cols = slice(half * (M // 2), (half + 1) * (M // 2))
+            y_g = sb(f"y_g{half}", [P, M // 2, PACK], BF16)
             copy_on(
                 nc,
                 engine,
-                y_g[:, cols, :].rearrange("p (c i) t -> p c t i", i=4),
+                y_g[:].rearrange("p (c i) t -> p c t i", i=4),
                 y[:, :, cols].rearrange("p t (c i) -> p c t i", i=4),
             )
-        y_c, y_s = quantize("y_q", y_g[:].rearrange("p n t -> p (n t)"), M)
-        nc.sync.dma_start(out=out_1[0].rearrange("p m t -> p (m t)").bitcast(I32), in_=y_c[:].bitcast(I32))
+            nc.vector.quantize_mx(out=y_c[:, cols].bitcast(FP8X4), scales=y_s[:, cols], in_=y_g[:].rearrange("p n t -> p (n t)"))
+            nc.sync.dma_start(out=words_out[:, cols], in_=y_c[:, cols].bitcast(I32))
         for q in range(4):
             queue = nc.scalar if q % 2 == 0 else nc.sync
             queue.dma_start(out=out_2[0, 4 * q : 4 * q + 4, :].bitcast(I32), in_=y_s[32 * q : 32 * q + 4, :].bitcast(I32))

@@ -18,34 +18,23 @@ ALU = mybir.AluOpType
 
 P = 128
 PACK = 4
+QUADRANTS = 4
 G = P * PACK
 W = 512
-KA = K // G
-HB = H // G
-JH = S // W
-V, A = "vector", "scalar"
-WARM = 0
-W1 = [[(A, A), (A, A), (V, A)], [(V, V), (V, V), (V, A)]]
-HG00 = V
-DEARLY = 2
-HG01 = V
-WB = [(V, V), (A, V)]
-EE = [[A, A, A, A], [A, A, A, A]]
-DE = [[V, V, A, A], [V, V, A, A]]
-SC = [V, V, V, V]
-
-
-def copy_on(nc, engine, out, in_):
-    if engine == "vector":
-        nc.vector.tensor_copy(out=out, in_=in_)
-    else:
-        nc.scalar.copy(out=out, in_=in_)
+PASSES = K // G
+GROUPS = H // G
+HALVES = S // W
+ENTRIES = 16
+RUN = 4
+WEIGHT_BUFS = 6
+D_SLICES_ON_VECTOR = 3
 
 
 def tile_list_victim_destination_scores_kernel(
     tc, tab_words, tab_scales, offs, pos1, pos2, w1, b1, wa_words, wa_scales, wb, limit, gm, gain, out_0, out_1, out_2
 ):
     nc = tc.nc
+    vector_copy, scalar_copy = nc.vector.tensor_copy, nc.scalar.copy
     with ExitStack() as ctx:
         keep = ctx.enter_context(tc.tile_pool(name="keep", bufs=1))
         psum = ctx.enter_context(tc.psum_pool(name="psum", bufs=8))
@@ -53,75 +42,62 @@ def tile_list_victim_destination_scores_kernel(
         def sb(name, shape, dtype, tag="", bufs=1):
             return keep.tile(shape, dtype, name=name, tag=tag or name, bufs=bufs, align_bytes=64)
 
-        offs_t = keep.tile([P, S // 16], U16, name="offs_t")
-        pos1_t = keep.tile([P, M // 16], U16, name="pos1_t")
-        pos2_t = keep.tile([P, M // 16], U16, name="pos2_t")
+        offs_t = keep.tile([P, S // ENTRIES], U16, name="offs_t")
+        pos1_t = keep.tile([P, M // ENTRIES], U16, name="pos1_t")
+        pos2_t = keep.tile([P, M // ENTRIES], U16, name="pos2_t")
 
-        if WARM:
-            warm = sb("warm", [P, 2], F32)
-            nc.gpsimd.memset(warm[:, 0:1], 0.0)
-            nc.scalar.activation(out=warm[:, 1:2], in_=warm[:, 0:1], func=ACT.Sigmoid)
         tab_s = sb("tab_s", [P, T], U8)
-        wa_s_raw = sb("wa_s_raw", [P, HB, N], U8)
-        nc.gpsimd.memset(tab_s[:].bitcast(I32), 0)
-        nc.vector.memset(wa_s_raw[:].bitcast(I32), 0)
-        for q in range(4):
-            nc.gpsimd.dma_start(
-                out=tab_s[32 * q : 32 * q + 4 * KA, :].bitcast(I32),
-                in_=tab_scales[:, 4 * q : 4 * q + 4, :].bitcast(I32),
-            )
+        wa_s_raw = sb("wa_s_raw", [P, GROUPS, N], U8)
+        nc.gpsimd.memset(tab_s[:, 0 : T // 2].bitcast(I32), 0)
+        nc.vector.memset(tab_s[:, T // 2 : T].bitcast(I32), 0)
+        nc.gpsimd.memset(wa_s_raw[:].bitcast(I32), 0)
 
         def load_rows(name, rows, slot):
             raw = sb(name, [P, PACK, W], F32, tag=f"raw{slot}")
             nc.sync.dma_start(out=raw[:], in_=rows.rearrange("(p j) c -> p j c", j=PACK))
             return raw
 
-        nc.sync.dma_start(offs_t[:], offs)
-        wa_w_raw = sb("wa_w_raw", [P, HB, 2 * N], U8)
-        nc.sync.dma_start(out=wa_w_raw[:].bitcast(I32), in_=wa_words.rearrange("b p c -> p b c").bitcast(I32))
         def load_table(a):
             words = sb(f"tab_w{a}", [P, T], U32)
             nc.sync.dma_start(out=words[:].bitcast(I32), in_=tab_words[a].rearrange("p t i -> p (t i)").bitcast(I32))
             return words
 
         def load_w1(b, a):
-            return load_rows(f"w1_raw_{b}_{a}", w1[a * G : (a + 1) * G, b * G : (b + 1) * G], b * KA + a)
+            return load_rows(f"w1_raw_{b}_{a}", w1[a * G : (a + 1) * G, b * G : (b + 1) * G], b * PASSES + a)
 
+        nc.sync.dma_start(offs_t[:], offs)
+        wa_w_raw = sb("wa_w_raw", [P, GROUPS, 2 * N], U8)
+        nc.sync.dma_start(out=wa_w_raw[:].bitcast(I32), in_=wa_words.rearrange("b p c -> p b c").bitcast(I32))
         tab_w = [load_table(0), load_table(1)]
-        w1_raw = {(0, 0): load_w1(0, 0), (0, 1): load_w1(0, 1)}
-        for q in range(4):
+        for q in range(QUADRANTS):
             nc.sync.dma_start(
-                out=wa_s_raw[32 * q : 32 * q + 4, :, :].bitcast(I32),
-                in_=wa_scales[:, 4 * q : 4 * q + 4, :].rearrange("b r n -> r b n").bitcast(I32),
+                out=tab_s[32 * q : 32 * q + PACK * PASSES, :].bitcast(I32),
+                in_=tab_scales[:, PACK * q : PACK * (q + 1), :].bitcast(I32),
+            )
+        w1_raw = {(0, 0): load_w1(0, 0), (0, 1): load_w1(0, 1)}
+        for q in range(QUADRANTS):
+            nc.sync.dma_start(
+                out=wa_s_raw[32 * q : 32 * q + PACK, :, :].bitcast(I32),
+                in_=wa_scales[:, PACK * q : PACK * (q + 1), :].rearrange("b r n -> r b n").bitcast(I32),
             )
         tab_w.append(load_table(2))
         w1_raw[0, 2] = load_w1(0, 2)
-        b1_t = sb("b1_t", [P, HB, PACK], F32)
-        nc.sync.dma_start(out=b1_t[:], in_=b1.rearrange("(b p t) -> p b t", b=HB, t=PACK))
-        for a in range(KA):
+        b1_t = sb("b1_t", [P, GROUPS, PACK], F32)
+        nc.sync.dma_start(out=b1_t[:], in_=b1.rearrange("(b p t) -> p b t", b=GROUPS, t=PACK))
+        for a in range(PASSES):
             w1_raw[1, a] = load_w1(1, a)
-        wb_raw = [load_rows(f"wb_raw_{b}", wb[b * G : (b + 1) * G, :], b) for b in range(HB)]
+        wb_raw = [load_rows(f"wb_raw_{b}", wb[b * G : (b + 1) * G, :], b) for b in range(GROUPS)]
         nc.sync.dma_start(pos1_t[:], pos1)
         nc.sync.dma_start(pos2_t[:], pos2)
         limit_t = sb("limit_t", [P, PACK], F32)
         gain_t = sb("gain_t", [P, PACK], F32)
         nc.sync.dma_start(out=limit_t[:], in_=limit.rearrange("(p t) -> p t", t=PACK))
         nc.sync.dma_start(out=gain_t[:], in_=gain.rearrange("(p t) -> p t", t=PACK))
-        gm_t = load_rows("gm_t", gm, 2)
+        gm_t = load_rows("gm_t", gm, GROUPS)
 
-        wa_w = sb("wa_w", [P, HB, PACK, P, 2], U8)
-        wa_s = sb("wa_s", [P, HB, PACK, P], U8)
+        wa_w = sb("wa_w", [P, GROUPS, PACK, P, 2], U8)
+        wa_s = sb("wa_s", [P, GROUPS, PACK, P], U8)
         nc.vector.tensor_copy(out=wa_w[:], in_=wa_w_raw[:].rearrange("p b (m t y) -> p b t m y", t=PACK, y=2))
-
-        def round_weight(name, raw, u, engine):
-            grouped = sb(f"{name}_g{u}", [P, 2, P, PACK], BF16, tag="w_g", bufs=6)
-            copy_on(
-                nc,
-                engine,
-                grouped[:].rearrange("p t m j -> p m j t"),
-                raw[:].rearrange("p j (m t) -> p m j t", t=PACK)[:, :, :, 2 * u : 2 * u + 2],
-            )
-            return grouped
 
         def quantize(name, grouped, width):
             codes = sb(f"{name}_c", [P, width], U32)
@@ -129,32 +105,42 @@ def tile_list_victim_destination_scores_kernel(
             nc.vector.quantize_mx(out=codes[:].bitcast(FP8X4), scales=scales[:], in_=grouped)
             return codes, scales
 
-        def quantize_weight(name, raw, engines):
-            grouped = [round_weight(name, raw, u, engines[u]) for u in range(2)]
-            return [quantize(f"{name}_{u}", grouped[u][:].rearrange("p t m j -> p (t m j)"), 2 * P) for u in range(2)]
+        def quantize_weight(name, raw, copies):
+            halves = []
+            for u in range(2):
+                grouped = sb(f"{name}_g{u}", [P, 2, P, PACK], BF16, tag="w_g", bufs=WEIGHT_BUFS)
+                copies[u](
+                    out=grouped[:].rearrange("p t m j -> p m j t"),
+                    in_=raw[:].rearrange("p j (m t) -> p m j t", t=PACK)[:, :, :, 2 * u : 2 * u + 2],
+                )
+                halves.append(grouped)
+            return [quantize(f"{name}_{u}", halves[u][:].rearrange("p t m j -> p (t m j)"), 2 * P) for u in range(2)]
 
         def slice_of(quantized, t):
             codes, scales = quantized[t // 2]
             cols = slice((t % 2) * P, (t % 2 + 1) * P)
             return codes[:, cols].bitcast(FP8X4), scales[:, cols]
 
-        def list_half(jh):
-            return offs_t[:, jh * (W // 16) : (jh + 1) * (W // 16)]
+        def interleave(copy, grouped, rows):
+            copy(
+                out=grouped.rearrange("p (c i) t -> p c t i", i=RUN),
+                in_=rows.rearrange("p t (c i) -> p c t i", i=RUN),
+            )
 
-        v_s = []
-        v_w = {}
+        def idx_half(jh):
+            return offs_t[:, jh * (W // ENTRIES) : (jh + 1) * (W // ENTRIES)]
 
-        def gather_scales(jh):
-            picked = sb(f"v_s{jh}", [P, W], U8)
-            nc.vector.tensor_copy(out=picked[:], in_=tab_s[:].indirect(list_half(jh)))
-            v_s.append(picked)
+        v_w, v_s, w1_q, h_acc, h_rows, h_q = {}, {}, {}, {}, {}, {}
 
-        def gather_words(a, jh):
-            picked = sb(f"v_w{a}_{jh}", [P, W], U32)
-            nc.vector.tensor_copy(out=picked[:], in_=tab_w[a][:].indirect(list_half(jh)))
-            v_w[a, jh] = picked
+        def gather_words(a):
+            for jh in range(HALVES):
+                v_w[a, jh] = sb(f"v_w{a}_{jh}", [P, W], U32)
+                nc.vector.tensor_copy(out=v_w[a, jh][:], in_=tab_w[a][:].indirect(idx_half(jh)))
 
-        h_acc = {}
+        def gather_scales():
+            for jh in range(HALVES):
+                v_s[jh] = sb(f"v_s{jh}", [P, W], U8)
+                nc.vector.tensor_copy(out=v_s[jh][:], in_=tab_s[:].indirect(idx_half(jh)))
 
         def stage1_pass(b, a, jh):
             for t in range(PACK):
@@ -166,68 +152,58 @@ def tile_list_victim_destination_scores_kernel(
                     lhsT=lhs,
                     lhsT_scale=lhs_s,
                     rhs=v_w[a, jh][:].bitcast(FP8X4),
-                    rhs_scale=v_s[jh][4 * a : P, :],
+                    rhs_scale=v_s[jh][PACK * a : P, :],
                     start=(a == 0),
-                    stop=(a == KA - 1),
+                    stop=(a == PASSES - 1),
                 )
 
-        h_rows = {}
-        h_q = {}
-
         def h_out(b, jh):
-            rows = sb(f"h_rows{b}_{jh}", [P, PACK, W], BF16)
+            h_rows[b, jh] = sb(f"h_rows{b}_{jh}", [P, PACK, W], BF16)
             for t in range(PACK):
-                nc.scalar.activation(out=rows[:, t, :], in_=h_acc[b, jh, t][:], func=ACT.Relu, bias=b1_t[:, b, t : t + 1])
-            h_rows[b, jh] = rows
+                nc.scalar.activation(
+                    out=h_rows[b, jh][:, t, :], in_=h_acc[b, jh, t][:], func=ACT.Relu, bias=b1_t[:, b, t : t + 1]
+                )
 
-        def interleave(name, rows, engine):
-            grouped = sb(name, [P, W, PACK], BF16, tag="x_g", bufs=2)
-            copy_on(
-                nc,
-                engine,
-                grouped[:].rearrange("p (c i) t -> p c t i", i=4),
-                rows[:].rearrange("p t (c i) -> p c t i", i=4),
-            )
-            return grouped[:].rearrange("p n t -> p (n t)")
+        def h_quantize(b, jh):
+            grouped = sb(f"h_g{b}_{jh}", [P, W, PACK], BF16, tag="h_g", bufs=2)
+            interleave(vector_copy, grouped[:], h_rows[b, jh][:])
+            h_q[b, jh] = quantize(f"h_q{b}_{jh}", grouped[:].rearrange("p n t -> p (n t)"), W)
 
-        def h_quantize(b, jh, engine):
-            h_q[b, jh] = quantize(f"h_q{b}_{jh}", interleave(f"h_g{b}_{jh}", h_rows[b, jh], engine), W)
-
-        w1_q = {}
-        for a in range(2):
-            for jh in range(JH):
-                gather_words(a, jh)
-        for jh in range(JH):
-            gather_scales(jh)
-        for a in range(KA):
-            if a == 2:
-                for jh in range(JH):
-                    gather_words(2, jh)
-            w1_q[0, a] = quantize_weight(f"w1_0_{a}", w1_raw[0, a], W1[0][a])
-            for jh in range(JH):
+        gather_words(0)
+        gather_words(1)
+        gather_scales()
+        for a in range(PASSES):
+            last = a == PASSES - 1
+            if last:
+                gather_words(a)
+            w1_q[0, a] = quantize_weight(f"w1_0_{a}", w1_raw[0, a], (vector_copy if last else scalar_copy, scalar_copy))
+            for jh in range(HALVES):
                 stage1_pass(0, a, jh)
         nc.vector.tensor_copy(out=wa_s[:], in_=wa_s_raw[:].rearrange("p b (m t) -> p b t m", t=PACK))
-        for jh in range(JH):
+        for jh in range(HALVES):
             h_out(0, jh)
-        for a in range(KA):
-            w1_q[1, a] = quantize_weight(f"w1_1_{a}", w1_raw[1, a], W1[1][a])
-        for jh in range(JH):
-            for a in range(KA):
+
+        for a in range(PASSES):
+            copy = scalar_copy if a == PASSES - 1 else vector_copy
+            w1_q[1, a] = quantize_weight(f"w1_1_{a}", w1_raw[1, a], (copy, copy))
+        for jh in range(HALVES):
+            for a in range(PASSES):
                 stage1_pass(1, a, jh)
-        h_out(1, 0)
-        h_quantize(0, 0, HG00)
-        h_quantize(1, 0, V)
-        h_out(1, 1)
-        h_quantize(0, 1, HG01)
-        h_quantize(1, 1, V)
-        wb_q = [quantize_weight(f"wb_{b}", wb_raw[b], WB[b]) for b in range(HB)]
+        for jh in range(HALVES):
+            h_out(1, jh)
+            for b in range(GROUPS):
+                h_quantize(b, jh)
+        wb_q = [
+            quantize_weight("wb_0", wb_raw[0], (vector_copy, vector_copy)),
+            quantize_weight("wb_1", wb_raw[1], (scalar_copy, vector_copy)),
+        ]
 
         e = [sb(f"e{t}", [P, S], F32) for t in range(PACK)]
         d = [sb(f"d{t}", [P, S], F32) for t in range(PACK)]
 
-        def stage2(whole, stationary, jh, t, engine):
+        def stage2(whole, stationary, jh, t, copy):
             acc = psum.tile([P, W], F32, name="bank")
-            for b in range(HB):
+            for b in range(GROUPS):
                 lhs, lhs_s = stationary(b, t)
                 nc.tensor.matmul_mx(
                     out=acc[:],
@@ -236,9 +212,9 @@ def tile_list_victim_destination_scores_kernel(
                     rhs=h_q[b, jh][0][:].bitcast(FP8X4),
                     rhs_scale=h_q[b, jh][1][:],
                     start=(b == 0),
-                    stop=(b == HB - 1),
+                    stop=(b == GROUPS - 1),
                 )
-            copy_on(nc, engine, whole[t][:, jh * W : (jh + 1) * W], acc[:])
+            copy(out=whole[t][:, jh * W : (jh + 1) * W], in_=acc[:])
 
         def wa_slice(b, t):
             return wa_w[:, b, t, :, :].rearrange("p m y -> p (m y)").bitcast(FP4X4), wa_s[:, b, t, :]
@@ -246,46 +222,50 @@ def tile_list_victim_destination_scores_kernel(
         def wb_slice(b, t):
             return slice_of(wb_q[b], t)
 
+        def d_copy(t):
+            return vector_copy if t < D_SLICES_ON_VECTOR else scalar_copy
+
         y = sb("y", [P, PACK, M], F32)
         y_out = out_0.rearrange("(p t) m -> p t m", t=PACK)
-        for t in range(PACK):
-            stage2(e, wa_slice, 0, t, EE[0][t])
-        looks = []
-        for t in range(PACK):
-            stage2(e, wa_slice, 1, t, EE[1][t])
-            look = sb(f"look{t}", [P, M], F32)
-            nc.scalar.activation(out=look[:], in_=e[t][:].indirect(pos1_t[:]), func=ACT.Sigmoid, bias=limit_t[:, t : t + 1])
-            looks.append(look)
-            if t < DEARLY:
-                for jh in range(JH):
-                    stage2(d, wb_slice, jh, t, DE[jh][t])
-        for t in range(PACK):
-            if t >= DEARLY:
-                for jh in range(JH):
-                    stage2(d, wb_slice, jh, t, DE[jh][t])
-            signed = sb(f"cost{t}", [P, M], F32, tag="cost", bufs=2)
-            nc.vector.tensor_tensor(out=signed[:], in0=looks[t][:], in1=gm_t[:, t, :], op=ALU.mult)
-            diff = sb(f"diff{t}", [P, M], F32, tag="diff", bufs=2)
-            nc.vector.tensor_tensor(out=diff[:], in0=d[t][:].indirect(pos2_t[:]), in1=signed[:], op=ALU.subtract)
-            if SC[t] == "vector":
-                nc.vector.tensor_scalar(out=y[:, t, :], in0=diff[:], scalar1=gain_t[:, t : t + 1], scalar2=None, op0=ALU.mult)
-            else:
-                nc.scalar.activation(out=y[:, t, :], in_=diff[:], func=ACT.Copy, scale=gain_t[:, t : t + 1])
+        looks, picks = {}, {}
+
+        def combine(t):
+            gain_col = gain_t[:, t : t + 1]
+            cost = sb(f"cost{t}", [P, M], F32, tag="cost", bufs=2)
+            nc.vector.scalar_tensor_tensor(
+                out=cost[:], in0=looks[t][:], scalar=gain_col, in1=gm_t[:, t, :], op0=ALU.mult, op1=ALU.mult
+            )
+            nc.vector.scalar_tensor_tensor(
+                out=y[:, t, :], in0=picks[t][:], scalar=gain_col, in1=cost[:], op0=ALU.mult, op1=ALU.subtract
+            )
             nc.sync.dma_start(out=y_out[:, t, :], in_=y[:, t, :])
+
+        for t in range(PACK):
+            stage2(e, wa_slice, 0, t, scalar_copy)
+        for t in range(PACK):
+            stage2(d, wb_slice, 0, t, d_copy(t))
+        for t in range(PACK):
+            stage2(e, wa_slice, 1, t, scalar_copy)
+            looks[t] = sb(f"look{t}", [P, M], F32)
+            nc.scalar.activation(out=looks[t][:], in_=e[t][:].indirect(pos1_t[:]), func=ACT.Sigmoid, bias=limit_t[:, t : t + 1])
+            stage2(d, wb_slice, 1, t, d_copy(t))
+            picks[t] = sb(f"pick{t}", [P, M], F32)
+            nc.vector.tensor_copy(out=picks[t][:], in_=d[t][:].indirect(pos2_t[:]))
+            if t > 0:
+                combine(t - 1)
+        combine(PACK - 1)
+
         y_c = sb("y_c", [P, M], U32)
         y_s = sb("y_s", [P, M], U8)
         words_out = out_1[0].rearrange("p m t -> p (m t)").bitcast(I32)
-        for half, engine in enumerate((V, A)):
+        for half, copy in enumerate((vector_copy, scalar_copy)):
             cols = slice(half * (M // 2), (half + 1) * (M // 2))
             y_g = sb(f"y_g{half}", [P, M // 2, PACK], BF16)
-            copy_on(
-                nc,
-                engine,
-                y_g[:].rearrange("p (c i) t -> p c t i", i=4),
-                y[:, :, cols].rearrange("p t (c i) -> p c t i", i=4),
-            )
+            interleave(copy, y_g[:], y[:, :, cols])
             nc.vector.quantize_mx(out=y_c[:, cols].bitcast(FP8X4), scales=y_s[:, cols], in_=y_g[:].rearrange("p n t -> p (n t)"))
             nc.sync.dma_start(out=words_out[:, cols], in_=y_c[:, cols].bitcast(I32))
-        for q in range(4):
+        for q in range(QUADRANTS):
             queue = nc.scalar if q % 2 == 0 else nc.sync
-            queue.dma_start(out=out_2[0, 4 * q : 4 * q + 4, :].bitcast(I32), in_=y_s[32 * q : 32 * q + 4, :].bitcast(I32))
+            queue.dma_start(
+                out=out_2[0, PACK * q : PACK * (q + 1), :].bitcast(I32), in_=y_s[32 * q : 32 * q + PACK, :].bitcast(I32)
+            )

@@ -27,6 +27,7 @@ HALVES = S // W
 ENTRIES = 16
 RUN = 4
 WEIGHT_BUFS = 6
+GAINS_ON_SCALAR = 3
 D_SLICES_ON_VECTOR = 3
 
 
@@ -184,8 +185,8 @@ def tile_list_victim_destination_scores_kernel(
             h_out(0, jh)
 
         for a in range(PASSES):
-            copy = scalar_copy if a == PASSES - 1 else vector_copy
-            w1_q[1, a] = quantize_weight(f"w1_1_{a}", w1_raw[1, a], (copy, copy))
+            second = scalar_copy if a == PASSES - 1 else vector_copy
+            w1_q[1, a] = quantize_weight(f"w1_1_{a}", w1_raw[1, a], (vector_copy, second))
         for jh in range(HALVES):
             for a in range(PASSES):
                 stage1_pass(1, a, jh)
@@ -227,18 +228,13 @@ def tile_list_victim_destination_scores_kernel(
 
         y = sb("y", [P, PACK, M], F32)
         y_out = out_0.rearrange("(p t) m -> p t m", t=PACK)
-        looks, picks = {}, {}
+        looks, diffs = {}, {}
 
-        def combine(t):
-            gain_col = gain_t[:, t : t + 1]
+        def difference(t):
             cost = sb(f"cost{t}", [P, M], F32, tag="cost", bufs=2)
-            nc.vector.scalar_tensor_tensor(
-                out=cost[:], in0=looks[t][:], scalar=gain_col, in1=gm_t[:, t, :], op0=ALU.mult, op1=ALU.mult
-            )
-            nc.vector.scalar_tensor_tensor(
-                out=y[:, t, :], in0=picks[t][:], scalar=gain_col, in1=cost[:], op0=ALU.mult, op1=ALU.subtract
-            )
-            nc.sync.dma_start(out=y_out[:, t, :], in_=y[:, t, :])
+            nc.vector.tensor_tensor(out=cost[:], in0=looks[t][:], in1=gm_t[:, t, :], op=ALU.mult)
+            diffs[t] = sb(f"diff{t}", [P, M], F32)
+            nc.vector.tensor_tensor(out=diffs[t][:], in0=d[t][:].indirect(pos2_t[:]), in1=cost[:], op=ALU.subtract)
 
         for t in range(PACK):
             stage2(e, wa_slice, 0, t, scalar_copy)
@@ -249,11 +245,16 @@ def tile_list_victim_destination_scores_kernel(
             looks[t] = sb(f"look{t}", [P, M], F32)
             nc.scalar.activation(out=looks[t][:], in_=e[t][:].indirect(pos1_t[:]), func=ACT.Sigmoid, bias=limit_t[:, t : t + 1])
             stage2(d, wb_slice, 1, t, d_copy(t))
-            picks[t] = sb(f"pick{t}", [P, M], F32)
-            nc.vector.tensor_copy(out=picks[t][:], in_=d[t][:].indirect(pos2_t[:]))
             if t > 0:
-                combine(t - 1)
-        combine(PACK - 1)
+                difference(t - 1)
+        difference(PACK - 1)
+        for t in range(PACK):
+            gain_col = gain_t[:, t : t + 1]
+            if t < GAINS_ON_SCALAR:
+                nc.scalar.activation(out=y[:, t, :], in_=diffs[t][:], func=ACT.Copy, scale=gain_col)
+            else:
+                nc.vector.tensor_scalar(out=y[:, t, :], in0=diffs[t][:], scalar1=gain_col, scalar2=None, op0=ALU.mult)
+            nc.sync.dma_start(out=y_out[:, t, :], in_=y[:, t, :])
 
         y_c = sb("y_c", [P, M], U32)
         y_s = sb("y_s", [P, M], U8)

@@ -47,6 +47,10 @@ def tile_list_victim_destination_scores_kernel(
         pos1_t = keep.tile([P, M // ENTRIES], U16, name="pos1_t")
         pos2_t = keep.tile([P, M // ENTRIES], U16, name="pos2_t")
 
+        warm = sb("warm", [P, 2], F32)
+        nc.gpsimd.memset(warm[:, 0:1], 0.0)
+        nc.scalar.activation(out=warm[:, 1:2], in_=warm[:, 0:1], func=ACT.Sigmoid)
+
         tab_s = sb("tab_s", [P, T], U8)
         wa_s_raw = sb("wa_s_raw", [P, GROUPS, N], U8)
         nc.gpsimd.memset(tab_s[:, 0 : T // 2].bitcast(I32), 0)

from contextlib import ExitStack

import concourse.mybir as mybir

K, T, S, H, N, M = 1536, 2048, 1024, 1024, 512, 512
FLOPS = 2 * K * H * S + 2 * 2 * H * N * S

F32 = mybir.dt.float32
BF16 = mybir.dt.bfloat16
I32 = mybir.dt.int32
U32 = mybir.dt.uint32
U16 = mybir.dt.uint16
U8 = mybir.dt.uint8
FP8X4 = mybir.dt.float8_e4m3fn_x4
FP4X4 = mybir.dt.float4_e2m1fn_x4
ACT = mybir.ActivationFunctionType
ALU = mybir.AluOpType

P = 128
PACK = 4
QUADRANTS = 4
G = P * PACK
W = 512
PASSES = K // G
GROUPS = H // G
HALVES = S // W
ENTRIES = 16
RUN = 4
WEIGHT_BUFS = 6
GAINS_ON_SCALAR = 3
D_SLICES_ON_VECTOR = 3


def tile_list_victim_destination_scores_kernel(
    tc, tab_words, tab_scales, offs, pos1, pos2, w1, b1, wa_words, wa_scales, wb, limit, gm, gain, out_0, out_1, out_2
):
    nc = tc.nc
    vector_copy, scalar_copy = nc.vector.tensor_copy, nc.scalar.copy
    with ExitStack() as ctx:
        keep = ctx.enter_context(tc.tile_pool(name="keep", bufs=1))
        psum = ctx.enter_context(tc.psum_pool(name="psum", bufs=8))

        def sb(name, shape, dtype, tag="", bufs=1):
            return keep.tile(shape, dtype, name=name, tag=tag or name, bufs=bufs, align_bytes=64)

        offs_t = keep.tile([P, S // ENTRIES], U16, name="offs_t")
        pos1_t = keep.tile([P, M // ENTRIES], U16, name="pos1_t")
        pos2_t = keep.tile([P, M // ENTRIES], U16, name="pos2_t")

        warm = sb("warm", [P, 2], F32)
        nc.gpsimd.memset(warm[:, 0:1], 0.0)
        nc.scalar.activation(out=warm[:, 1:2], in_=warm[:, 0:1], func=ACT.Sigmoid)

        tab_s = sb("tab_s", [P, T], U8)
        wa_s_raw = sb("wa_s_raw", [P, GROUPS, N], U8)
        nc.gpsimd.memset(tab_s[:, 0 : T // 2].bitcast(I32), 0)
        nc.vector.memset(tab_s[:, T // 2 : T].bitcast(I32), 0)
        nc.gpsimd.memset(wa_s_raw[:].bitcast(I32), 0)

        def load_rows(name, rows, slot):
            raw = sb(name, [P, PACK, W], F32, tag=f"raw{slot}")
            nc.sync.dma_start(out=raw[:], in_=rows.rearrange("(p j) c -> p j c", j=PACK))
            return raw

        def load_table(a):
            words = sb(f"tab_w{a}", [P, T], U32)
            nc.sync.dma_start(out=words[:].bitcast(I32), in_=tab_words[a].rearrange("p t i -> p (t i)").bitcast(I32))
            return words

        def load_w1(b, a):
            return load_rows(f"w1_raw_{b}_{a}", w1[a * G : (a + 1) * G, b * G : (b + 1) * G], b * PASSES + a)

        nc.sync.dma_start(offs_t[:], offs)
        wa_w_raw = sb("wa_w_raw", [P, GROUPS, 2 * N], U8)
        nc.sync.dma_start(out=wa_w_raw[:].bitcast(I32), in_=wa_words.rearrange("b p c -> p b c").bitcast(I32))
        tab_w = [load_table(0), load_table(1)]
        for q in range(QUADRANTS):
            nc.sync.dma_start(
                out=tab_s[32 * q : 32 * q + PACK * PASSES, :].bitcast(I32),
                in_=tab_scales[:, PACK * q : PACK * (q + 1), :].bitcast(I32),
            )
        w1_raw = {(0, 0): load_w1(0, 0), (0, 1): load_w1(0, 1)}
        for q in range(QUADRANTS):
            nc.sync.dma_start(
                out=wa_s_raw[32 * q : 32 * q + PACK, :, :].bitcast(I32),
                in_=wa_scales[:, PACK * q : PACK * (q + 1), :].rearrange("b r n -> r b n").bitcast(I32),
            )
        tab_w.append(load_table(2))
        w1_raw[0, 2] = load_w1(0, 2)
        b1_t = sb("b1_t", [P, GROUPS, PACK], F32)
        nc.sync.dma_start(out=b1_t[:], in_=b1.rearrange("(b p t) -> p b t", b=GROUPS, t=PACK))
        for a in range(PASSES):
            w1_raw[1, a] = load_w1(1, a)
        wb_raw = [load_rows(f"wb_raw_{b}", wb[b * G : (b + 1) * G, :], b) for b in range(GROUPS)]
        nc.sync.dma_start(pos1_t[:], pos1)
        nc.sync.dma_start(pos2_t[:], pos2)
        limit_t = sb("limit_t", [P, PACK], F32)
        gain_t = sb("gain_t", [P, PACK], F32)
        nc.sync.dma_start(out=limit_t[:], in_=limit.rearrange("(p t) -> p t", t=PACK))
        nc.sync.dma_start(out=gain_t[:], in_=gain.rearrange("(p t) -> p t", t=PACK))
        gm_t = load_rows("gm_t", gm, GROUPS)

        wa_w = sb("wa_w", [P, GROUPS, PACK, P, 2], U8)
        wa_s = sb("wa_s", [P, GROUPS, PACK, P], U8)
        nc.vector.tensor_copy(out=wa_w[:], in_=wa_w_raw[:].rearrange("p b (m t y) -> p b t m y", t=PACK, y=2))

        def quantize(name, grouped, width):
            codes = sb(f"{name}_c", [P, width], U32)
            scales = sb(f"{name}_s", [P, width], U8)
            nc.vector.quantize_mx(out=codes[:].bitcast(FP8X4), scales=scales[:], in_=grouped)
            return codes, scales

        def quantize_weight(name, raw, copies):
            halves = []
            for u in range(2):
                grouped = sb(f"{name}_g{u}", [P, 2, P, PACK], BF16, tag="w_g", bufs=WEIGHT_BUFS)
                copies[u](
                    out=grouped[:].rearrange("p t m j -> p m j t"),
                    in_=raw[:].rearrange("p j (m t) -> p m j t", t=PACK)[:, :, :, 2 * u : 2 * u + 2],
                )
                halves.append(grouped)
            return [quantize(f"{name}_{u}", halves[u][:].rearrange("p t m j -> p (t m j)"), 2 * P) for u in range(2)]

        def slice_of(quantized, t):
            codes, scales = quantized[t // 2]
            cols = slice((t % 2) * P, (t % 2 + 1) * P)
            return codes[:, cols].bitcast(FP8X4), scales[:, cols]

        def interleave(copy, grouped, rows):
            copy(
                out=grouped.rearrange("p (c i) t -> p c t i", i=RUN),
                in_=rows.rearrange("p t (c i) -> p c t i", i=RUN),
            )

        def idx_half(jh):
            return offs_t[:, jh * (W // ENTRIES) : (jh + 1) * (W // ENTRIES)]

        v_w, v_s, w1_q, h_acc, h_rows, h_q = {}, {}, {}, {}, {}, {}

        def gather_words(a):
            for jh in range(HALVES):
                v_w[a, jh] = sb(f"v_w{a}_{jh}", [P, W], U32)
                nc.vector.tensor_copy(out=v_w[a, jh][:], in_=tab_w[a][:].indirect(idx_half(jh)))

        def gather_scales():
            for jh in range(HALVES):
                v_s[jh] = sb(f"v_s{jh}", [P, W], U8)
                nc.vector.tensor_copy(out=v_s[jh][:], in_=tab_s[:].indirect(idx_half(jh)))

        def stage1_pass(b, a, jh):
            for t in range(PACK):
                if a == 0:
                    h_acc[b, jh, t] = psum.tile([P, W], F32, name="bank")
                lhs, lhs_s = slice_of(w1_q[b, a], t)
                nc.tensor.matmul_mx(
                    out=h_acc[b, jh, t][:],
                    lhsT=lhs,
                    lhsT_scale=lhs_s,
                    rhs=v_w[a, jh][:].bitcast(FP8X4),
                    rhs_scale=v_s[jh][PACK * a : P, :],
                    start=(a == 0),
                    stop=(a == PASSES - 1),
                )

        def h_out(b, jh):
            h_rows[b, jh] = sb(f"h_rows{b}_{jh}", [P, PACK, W], BF16)
            for t in range(PACK):
                nc.scalar.activation(
                    out=h_rows[b, jh][:, t, :], in_=h_acc[b, jh, t][:], func=ACT.Relu, bias=b1_t[:, b, t : t + 1]
                )

        def h_quantize(b, jh):
            grouped = sb(f"h_g{b}_{jh}", [P, W, PACK], BF16, tag="h_g", bufs=2)
            interleave(vector_copy, grouped[:], h_rows[b, jh][:])
            h_q[b, jh] = quantize(f"h_q{b}_{jh}", grouped[:].rearrange("p n t -> p (n t)"), W)

        gather_words(0)
        gather_words(1)
        gather_scales()
        for a in range(PASSES):
            last = a == PASSES - 1
            if last:
                gather_words(a)
            w1_q[0, a] = quantize_weight(f"w1_0_{a}", w1_raw[0, a], (vector_copy if last else scalar_copy, scalar_copy))
            for jh in range(HALVES):
                stage1_pass(0, a, jh)
        nc.vector.tensor_copy(out=wa_s[:], in_=wa_s_raw[:].rearrange("p b (m t) -> p b t m", t=PACK))
        for jh in range(HALVES):
            h_out(0, jh)

        for a in range(PASSES):
            second = scalar_copy if a == PASSES - 1 else vector_copy
            w1_q[1, a] = quantize_weight(f"w1_1_{a}", w1_raw[1, a], (vector_copy, second))
        for jh in range(HALVES):
            for a in range(PASSES):
                stage1_pass(1, a, jh)
        for jh in range(HALVES):
            h_out(1, jh)
            for b in range(GROUPS):
                h_quantize(b, jh)
        wb_q = [
            quantize_weight("wb_0", wb_raw[0], (vector_copy, vector_copy)),
            quantize_weight("wb_1", wb_raw[1], (scalar_copy, vector_copy)),
        ]

        e = [sb(f"e{t}", [P, S], F32) for t in range(PACK)]
        d = [sb(f"d{t}", [P, S], F32) for t in range(PACK)]

        def stage2(whole, stationary, jh, t, copy):
            acc = psum.tile([P, W], F32, name="bank")
            for b in range(GROUPS):
                lhs, lhs_s = stationary(b, t)
                nc.tensor.matmul_mx(
                    out=acc[:],
                    lhsT=lhs,
                    lhsT_scale=lhs_s,
                    rhs=h_q[b, jh][0][:].bitcast(FP8X4),
                    rhs_scale=h_q[b, jh][1][:],
                    start=(b == 0),
                    stop=(b == GROUPS - 1),
                )
            copy(out=whole[t][:, jh * W : (jh + 1) * W], in_=acc[:])

        def wa_slice(b, t):
            return wa_w[:, b, t, :, :].rearrange("p m y -> p (m y)").bitcast(FP4X4), wa_s[:, b, t, :]

        def wb_slice(b, t):
            return slice_of(wb_q[b], t)

        def d_copy(t):
            return vector_copy if t < D_SLICES_ON_VECTOR else scalar_copy

        y = sb("y", [P, PACK, M], F32)
        y_out = out_0.rearrange("(p t) m -> p t m", t=PACK)
        looks, diffs = {}, {}

        def difference(t):
            cost = sb(f"cost{t}", [P, M], F32, tag="cost", bufs=2)
            nc.vector.tensor_tensor(out=cost[:], in0=looks[t][:], in1=gm_t[:, t, :], op=ALU.mult)
            diffs[t] = sb(f"diff{t}", [P, M], F32)
            nc.vector.tensor_tensor(out=diffs[t][:], in0=d[t][:].indirect(pos2_t[:]), in1=cost[:], op=ALU.subtract)

        for t in range(PACK):
            stage2(e, wa_slice, 0, t, scalar_copy)
        for t in range(PACK):
            stage2(d, wb_slice, 0, t, d_copy(t))
        for t in range(PACK):
            stage2(e, wa_slice, 1, t, scalar_copy)
            looks[t] = sb(f"look{t}", [P, M], F32)
            nc.scalar.activation(out=looks[t][:], in_=e[t][:].indirect(pos1_t[:]), func=ACT.Sigmoid, bias=limit_t[:, t : t + 1])
            stage2(d, wb_slice, 1, t, d_copy(t))
            if t > 0:
                difference(t - 1)
        difference(PACK - 1)
        for t in range(PACK):
            gain_col = gain_t[:, t : t + 1]
            if t < GAINS_ON_SCALAR:
                nc.scalar.activation(out=y[:, t, :], in_=diffs[t][:], func=ACT.Copy, scale=gain_col)
            else:
                nc.vector.tensor_scalar(out=y[:, t, :], in0=diffs[t][:], scalar1=gain_col, scalar2=None, op0=ALU.mult)
            nc.sync.dma_start(out=y_out[:, t, :], in_=y[:, t, :])

        y_c = sb("y_c", [P, M], U32)
        y_s = sb("y_s", [P, M], U8)
        words_out = out_1[0].rearrange("p m t -> p (m t)").bitcast(I32)
        for half, copy in enumerate((vector_copy, scalar_copy)):
            cols = slice(half * (M // 2), (half + 1) * (M // 2))
            y_g = sb(f"y_g{half}", [P, M // 2, PACK], BF16)
            interleave(copy, y_g[:], y[:, :, cols])
            nc.vector.quantize_mx(out=y_c[:, cols].bitcast(FP8X4), scales=y_s[:, cols], in_=y_g[:].rearrange("p n t -> p (n t)"))
            nc.sync.dma_start(out=words_out[:, cols], in_=y_c[:, cols].bitcast(I32))
        for q in range(QUADRANTS):
            queue = nc.scalar if q % 2 == 0 else nc.sync
            queue.dma_start(
                out=out_2[0, PACK * q : PACK * (q + 1), :].bitcast(I32), in_=y_s[32 * q : 32 * q + PACK, :].bitcast(I32)
            )
